import numpy as np
import ml_dtypes


def mxq(x, axis, fmt="e4m3"):
    dtype, down = {"e4m3": (ml_dtypes.float8_e4m3fn, 7), "e5m2": (ml_dtypes.float8_e5m2, 14)}[fmt]
    v = np.moveaxis(np.asarray(x, np.float32).astype(ml_dtypes.bfloat16).astype(np.float64), axis, -1)
    blocks = v.reshape(v.shape[:-1] + (-1, 32))
    amax = np.abs(blocks).max(-1, keepdims=True)
    byte = np.maximum(np.where(amax > 0, np.frexp(amax)[1] - 1 + 127, 0) - down, 1)
    scale = np.exp2(byte - 127.0)
    codes = (blocks / scale).astype(np.float32).astype(dtype).astype(np.float64)
    return np.moveaxis((codes * scale).reshape(v.shape), -1, axis)


WIDE = False


def mx_kscale(k):
    if not WIDE:
        return np.ones(k)
    levels = np.array([10, -10, 5, -5, 0])
    if k % 512:
        return np.exp2(np.random.permutation(np.resize(levels, k // 32))).repeat(32)
    a = np.empty((k // 512, 16))
    for p in range(k // 512):
        a[p, :8] = np.random.permutation(np.resize(levels, 8))
        for g in range(8):
            far = levels[np.abs(levels - a[p, g]) >= 10]
            a[p, g + 8] = far[np.random.randint(len(far))]
    return np.exp2(a.ravel()).repeat(32)


def f64(x):
    return np.asarray(x).astype(np.float64)


def striped(idx):
    return np.tile(idx.reshape(-1, 16).T, (8, 1)).astype(np.uint16)


def unstriped(offs):
    return offs[:16].T.reshape(-1).astype(np.int64)


E2M1 = np.array([0.0, 0.5, 1.0, 1.5, 2.0, 3.0, 4.0, 6.0, -0.0, -0.5, -1.0, -1.5, -2.0, -3.0, -4.0, -6.0])


def pack_weight(w, fmt):
    k, n = w.shape
    w = f64(np.asarray(w, np.float32).astype(ml_dtypes.bfloat16)).reshape(k // 32, 32, n)
    amax = np.abs(w).max(1)
    if fmt == "e4m3":
        byte = np.frexp(amax)[1] - 1 + 127 - 7
    else:
        mant, ex = np.frexp(amax / 6.0)
        byte = np.where(mant > 0.5, ex, ex - 1) + 127
    byte = np.clip(np.where(amax > 0, byte, 1), 1, 254)
    scaled = (w * np.exp2(127.0 - byte)[:, None, :]).reshape(k, n).astype(np.float32)
    by_word = np.ascontiguousarray(scaled.reshape(k // 512, 128, 4, n).transpose(0, 1, 3, 2))
    if fmt == "e4m3":
        words = by_word.astype(ml_dtypes.float8_e4m3fn).view(np.uint8)
    else:
        c = by_word.astype(ml_dtypes.float4_e2m1fn).view(np.uint8) & 0xF
        words = (c[..., 0::2] | (c[..., 1::2] << 4)).reshape(k // 512, 128, 2 * n)
    return np.ascontiguousarray(words), np.ascontiguousarray(byte.astype(np.uint8).reshape(k // 512, 16, n))


def unpack_weight(words, scales, fmt):
    g, _, n = scales.shape
    words = np.ascontiguousarray(words).reshape(g, 128, n, -1)
    if fmt == "e4m3":
        vals = words.view(ml_dtypes.float8_e4m3fn).astype(np.float64)
    else:
        nib = np.empty((g, 128, n, 4), np.uint8)
        nib[..., 0::2] = words & 0xF
        nib[..., 1::2] = words >> 4
        vals = E2M1[nib]
    vals = vals * np.repeat(np.exp2(scales.astype(np.float64) - 127.0), 8, axis=1)[..., None]
    return vals.transpose(0, 1, 3, 2).reshape(g * 512, n)


def gelu(v):
    return 0.5 * v * (1.0 + np.tanh(np.sqrt(2.0 / np.pi) * (v + 0.044715 * v**3)))


K, T, S, H, T2, P, N = 1024, 4096, 1024, 1024, 2048, 512, 512

def setup_inputs():
    n = np.random.standard_normal
    s = mx_kscale(K)[:, None]
    u = mx_kscale(H)[:, None]
    tab_words, tab_scales = pack_weight(n((K, T)) * s, "e4m3")
    w1 = (1.5 * n((K, H)) / np.sqrt(K) / s).astype(np.float32)
    gain = (1.2 * np.exp(0.3 * n(H)) * u[:, 0]).astype(np.float32)
    season = (0.7 * n((H, S)) * u).astype(np.float32)
    page0 = (n((H, T2)) * u).astype(np.float32)
    wgs = np.exp(0.3 * n((128, S))).astype(np.float32)
    rate = np.exp(0.5 * n(H)).astype(np.float32)
    w4_words, w4_scales = pack_weight(n((H, N)) / np.sqrt(H) / u, "e2m1")
    perm = np.random.permutation(T2)
    return {"tab_words": tab_words, "tab_scales": tab_scales, "w1": w1, "gain": gain,
            "season": season, "page0": page0, "wgs": wgs, "rate": rate,
            "w4_words": w4_words, "w4_scales": w4_scales,
            "offs": striped(np.random.permutation(T)[:S]),
            "offs2": striped(np.random.permutation(T2)[:S]),
            "offs3": striped(perm[:P]), "offs4": striped(perm[P:2 * P])}

def reference(tab_words, tab_scales, w1, gain, season, page0, wgs, rate,
              w4_words, w4_scales, offs, offs2, offs3, offs4):
    v = unpack_weight(tab_words, tab_scales, "e4m3")[:, unstriped(offs)]
    e = mxq(f64(w1), 0, "e4m3").T @ v
    h = f64(gain)[:, None] * np.tanh(e) + f64(season)
    page = f64(page0).copy()
    page[:, unstriped(offs2)] = np.tile(f64(wgs), (H // 128, 1)) * h
    a = page[:, unstriped(offs3)]
    b = page[:, unstriped(offs4)]
    top = np.maximum(a, b)
    page[:, unstriped(offs3)] = top
    page[:, unstriped(offs4)] = f64(rate)[:, None] * (b - top)
    w4 = unpack_weight(w4_words, w4_scales, "e2m1")
    return w4.T @ mxq(page, 0, "e4m3")

@@ -1,0 +1,295 @@
+from contextlib import ExitStack
+
+import concourse.mybir as mybir
+
+K, T, S, H, T2, PAIRS, N = 1024, 4096, 1024, 1024, 2048, 512, 512
+FLOPS = 2 * K * H * S + 2 * H * N * T2
+
+F32 = mybir.dt.float32
+BF16 = mybir.dt.bfloat16
+I32 = mybir.dt.int32
+U32 = mybir.dt.uint32
+U16 = mybir.dt.uint16
+U8 = mybir.dt.uint8
+FP8X4 = mybir.dt.float8_e4m3fn_x4
+FP4X4 = mybir.dt.float4_e2m1fn_x4
+ALU = mybir.AluOpType
+ACT = mybir.ActivationFunctionType
+
+P = 128
+PACK = 4
+K_PASS = P * PACK
+BANK = 512
+QUADS = 4
+BYTE_ORDER = (0, 2, 1, 3)
+SLICES = [(b, i) for b in range(H // K_PASS) for i in BYTE_ORDER]
+CHUNKS = T2 // BANK
+N_TILES = N // P
+VECTOR_BANKS = 3
+
+
+def tile_list_quota_swap_scores_kernel(
+    tc, tab_words, tab_scales, w1, gain, season, page0, wgs, rate,
+    w4_words, w4_scales, offs, offs2, offs3, offs4, out,
+):
+    nc = tc.nc
+    passes = K // K_PASS
+    last = len(SLICES) - 1
+
+    with ExitStack() as ctx:
+        keep = ctx.enter_context(tc.tile_pool(name="keep", bufs=1))
+        ring = ctx.enter_context(tc.tile_pool(name="ring", bufs=2))
+        psum = ctx.enter_context(tc.psum_pool(name="psum", bufs=8))
+
+        def load_list(src, name):
+            tile = keep.tile(list(src.shape), U16, name=name)
+            nc.sync.dma_start(tile[:], src)
+            return tile
+
+        table_scales = keep.tile([P, T], U8, name="table_scales", align_bytes=64)
+        nc.vector.memset(table_scales[:].bitcast(I32), 0)
+        for q in range(QUADS):
+            nc.gpsimd.dma_start(
+                table_scales[32 * q : 32 * q + 4 * passes, :].bitcast(I32),
+                tab_scales[:, 4 * q : 4 * q + 4, :].bitcast(I32),
+            )
+        gains = keep.tile([P, passes, PACK], F32, name="gains")
+        nc.scalar.dma_start(gains[:], gain.rearrange("(b p i) -> p b i", p=P, i=PACK))
+        rates = keep.tile([P, passes, PACK], F32, name="rates")
+        nc.scalar.dma_start(rates[:], rate.rearrange("(b p i) -> p b i", p=P, i=PACK))
+        w4_planes = keep.tile([P, passes * N], U8, name="w4_planes", align_bytes=64)
+        nc.vector.memset(w4_planes[:].bitcast(I32), 0)
+
+        list1 = load_list(offs, "list1")
+
+        w1_codes, w1_planes = {}, {}
+
+        def load_w1(a, b):
+            raw = ring.tile([P, PACK, K_PASS], F32, name="w1_raw")
+            nc.sync.dma_start(
+                raw[:],
+                w1[a * K_PASS : (a + 1) * K_PASS, b * K_PASS : (b + 1) * K_PASS].rearrange("(p j) c -> p j c", j=PACK),
+            )
+            return raw
+
+        def quantise_w1(a, b, raw):
+            woven = ring.tile([P, K_PASS * PACK], BF16, name="w1_woven", align_bytes=64)
+            nc.scalar.copy(
+                woven[:].rearrange("p (i m j) -> p m i j", i=PACK, j=PACK),
+                raw[:].rearrange("p j (m i) -> p m i j", i=PACK),
+            )
+            w1_codes[a, b] = keep.tile([P, K_PASS], U32, name="w1_codes_%d%d" % (a, b), align_bytes=64)
+            w1_planes[a, b] = keep.tile([P, K_PASS], U8, name="w1_planes_%d%d" % (a, b), align_bytes=64)
+            nc.vector.quantize_mx(w1_codes[a, b][:].bitcast(FP8X4), w1_planes[a, b][:], woven[:])
+
+        raws = [load_w1(a, 0) for a in range(passes)]
+        table = []
+        for a in range(passes):
+            words = ring.tile([P, T], U32, name="table_words", tag="wide", align_bytes=64)
+            nc.sync.dma_start(words[:].bitcast(I32), tab_words[a].rearrange("p t i -> p (t i)").bitcast(I32))
+            table.append(words)
+        list2 = load_list(offs2, "list2")
+
+        seasons, pages, weights = {}, {}, {}
+
+        def rows(src, c):
+            b, i = SLICES[c]
+            return src.rearrange("(b p i) s -> b i p s", p=P, i=PACK)[b, i]
+
+        def load_slice(c):
+            b, i = SLICES[c]
+            seasons[c] = ring.tile([P, S], F32, name="season_rows", bufs=3)
+            nc.sync.dma_start(seasons[c][:], rows(season, c))
+            if b == 0:
+                weights[i] = keep.tile([P, S], F32, name="wgs_rows_%d" % i)
+                for q in range(QUADS):
+                    nc.sync.dma_start(
+                        weights[i][32 * q : 32 * q + 32, :], wgs.rearrange("(m i) s -> i m s", i=PACK)[i]
+                    )
+            pages[c] = ring.tile([P, T2], F32, name="page", bufs=5)
+            nc.sync.dma_start(pages[c][:], rows(page0, c))
+
+        load_slice(0)
+        list3 = load_list(offs3, "list3")
+        list4 = load_list(offs4, "list4")
+        load_slice(1)
+        load_slice(2)
+
+        for a in range(passes):
+            quantise_w1(a, 0, raws[a])
+
+        picked_scales = keep.tile([P, S], U8, name="picked_scales", align_bytes=64)
+        nc.vector.tensor_copy(picked_scales[:], table_scales[:].indirect(list1[:]))
+        picked = [keep.tile([P, S], U32, name="picked_words_%d" % a, align_bytes=64) for a in range(passes)]
+        nc.vector.tensor_copy(picked[0][:], table[0][:].indirect(list1[:]))
+        halves = [slice(u * BANK, (u + 1) * BANK) for u in range(S // BANK)]
+        list_halves = [slice(u * BANK // 16, (u + 1) * BANK // 16) for u in range(S // BANK)]
+        for cols, lcols in zip(halves, list_halves):
+            nc.vector.tensor_copy(picked[1][:, cols], table[1][:].indirect(list1[:, lcols]))
+
+        tanhs, hs, sides3, sides4, tops, scaled4, scaled_tops = {}, {}, {}, {}, {}, {}, {}
+
+        def first_product(c):
+            b, i = SLICES[c]
+            tanhs[c] = ring.tile([P, S], F32, name="tanh_rows")
+            for cols in halves:
+                bank = psum.tile([P, BANK], F32, name="bank")
+                for a in range(passes):
+                    nc.tensor.matmul_mx(
+                        bank[:],
+                        lhsT=w1_codes[a, b][:, i * P : (i + 1) * P].bitcast(FP8X4),
+                        lhsT_scale=w1_planes[a, b][:, i * P : (i + 1) * P],
+                        rhs=picked[a][:, cols].bitcast(FP8X4),
+                        rhs_scale=picked_scales[4 * a : P, cols],
+                        start=(a == 0),
+                        stop=(a == passes - 1),
+                    )
+                nc.scalar.activation(tanhs[c][:, cols], bank[:], ACT.Tanh)
+
+        def make_h(c, cols):
+            b, i = SLICES[c]
+            nc.vector.scalar_tensor_tensor(
+                hs[c][:, cols], tanhs[c][:, cols], gains[:, b, i : i + 1], seasons[c][:, cols], ALU.mult, ALU.add
+            )
+
+        def put_h(c, cols, lcols):
+            i = SLICES[c][1]
+            nc.vector.tensor_tensor(
+                pages[c][:].indirect(list2[:, lcols]), hs[c][:, cols], weights[i][:, cols], ALU.mult
+            )
+
+        def fetch(c):
+            b, i = SLICES[c]
+            sides3[c] = ring.tile([P, PAIRS], F32, name="side3")
+            nc.vector.tensor_copy(sides3[c][:], pages[c][:].indirect(list3[:]))
+            sides4[c] = ring.tile([P, PAIRS], F32, name="side4")
+            nc.vector.tensor_copy(sides4[c][:], pages[c][:].indirect(list4[:]))
+            scaled4[c] = ring.tile([P, PAIRS], F32, name="scaled4")
+            nc.scalar.activation(scaled4[c][:], sides4[c][:], ACT.Copy, scale=rates[:, b, i : i + 1])
+
+        def larger(c):
+            b, i = SLICES[c]
+            tops[c] = ring.tile([P, PAIRS], F32, name="top")
+            nc.vector.tensor_tensor(tops[c][:], sides3[c][:], sides4[c][:], ALU.max)
+            scaled_tops[c] = ring.tile([P, PAIRS], F32, name="scaled_top")
+            nc.scalar.activation(scaled_tops[c][:], tops[c][:], ACT.Copy, scale=minus_rates[:, b, i : i + 1])
+
+        def put_top(c):
+            nc.vector.tensor_copy(pages[c][:].indirect(list3[:]), tops[c][:])
+
+        def put_shortfall(c):
+            nc.vector.tensor_tensor(pages[c][:].indirect(list4[:]), scaled4[c][:], scaled_tops[c][:], ALU.add)
+
+        woven_page, page_codes, page_planes = {}, {}, {}
+
+        def weave(c, q):
+            b, i = SLICES[c]
+            if i == BYTE_ORDER[0]:
+                woven_page[b, q] = keep.tile(
+                    [P, BANK, PACK], BF16, name="woven_page", tag="woven_page_%d" % q, align_bytes=64
+                )
+            src = pages[c][:, q * BANK : (q + 1) * BANK]
+            if c == last:
+                nc.vector.tensor_copy(woven_page[b, q][:, :, i], src)
+            else:
+                nc.scalar.copy(woven_page[b, q][:, :, i], src)
+
+        def quantise_page(b, q):
+            page_codes[b, q] = keep.tile([P, BANK], U32, name="page_codes_%d%d" % (b, q), align_bytes=64)
+            page_planes[b, q] = keep.tile([P, BANK], U8, name="page_planes_%d%d" % (b, q), align_bytes=64)
+            nc.vector.quantize_mx(
+                page_codes[b, q][:].bitcast(FP8X4),
+                page_planes[b, q][:],
+                woven_page[b, q][:].rearrange("p t i -> p (t i)"),
+            )
+
+        w4_codes = keep.tile([P, passes, 2 * N], U8, name="w4_codes", align_bytes=64)
+        score_banks = {}
+
+        def second_product(b, q, n):
+            if b == 0:
+                score_banks[q, n] = psum.tile([P, BANK], F32, name="bank")
+            nc.tensor.matmul_mx(
+                score_banks[q, n][:],
+                lhsT=w4_codes[:, b, 2 * P * n : 2 * P * (n + 1)].bitcast(FP4X4),
+                lhsT_scale=w4_planes[:, b * N + P * n : b * N + P * (n + 1)],
+                rhs=page_codes[b, q][:].bitcast(FP8X4),
+                rhs_scale=page_planes[b, q][:],
+                start=(b == 0),
+                stop=(b == passes - 1),
+            )
+
+        first_product(0)
+        first_product(1)
+        minus_rates = keep.tile([P, passes, PACK], F32, name="minus_rates")
+        nc.scalar.mul(minus_rates[:], rates[:], -1.0)
+
+        hs[0] = ring.tile([P, S], F32, name="h_rows")
+        for cols in halves:
+            make_h(0, cols)
+        for cols, lcols in zip(halves, list_halves):
+            put_h(0, cols, lcols)
+
+        whole = slice(0, S)
+        whole_list = slice(0, S // 16)
+        early_chunks = 8 // N_TILES
+        for c in range(-1, last + 1):
+            if c + 4 <= last:
+                load_slice(c + 4)
+            if c == -1:
+                raws = [load_w1(a, 1) for a in range(passes)]
+                nc.sync.dma_start(
+                    w4_codes[:].bitcast(I32), w4_words.bitcast(I32).rearrange("a p n -> p a n")
+                )
+            if c == 1:
+                for q in range(QUADS):
+                    nc.sync.dma_start(
+                        w4_planes[32 * q : 32 * q + 4, :].bitcast(I32).rearrange("r (a n) -> r a n", a=passes),
+                        w4_scales[:, 4 * q : 4 * q + 4, :].bitcast(I32).rearrange("a r n -> r a n"),
+                    )
+            if c >= 0:
+                put_top(c)
+            if c + 1 <= last:
+                fetch(c + 1)
+            if c + 2 <= last:
+                hs[c + 2] = ring.tile([P, S], F32, name="h_rows")
+                make_h(c + 2, whole)
+            if c >= 0:
+                put_shortfall(c)
+            if c + 1 <= last:
+                larger(c + 1)
+            if c == 0:
+                for a in range(passes):
+                    quantise_w1(a, 1, raws[a])
+            if c + 3 <= last:
+                first_product(c + 3)
+            if c == PACK:
+                for q in range(CHUNKS):
+                    quantise_page(0, q)
+            if c + 2 <= last:
+                put_h(c + 2, whole, whole_list)
+            if 0 <= c < last:
+                for q in range(CHUNKS):
+                    weave(c, q)
+            if c == PACK + 1:
+                for q in range(early_chunks):
+                    for n in range(N_TILES):
+                        second_product(0, q, n)
+
+        staged = [
+            ring.tile([P, 2 * N_TILES, BANK], F32, name="staged", tag="wide", align_bytes=64) for u in range(2)
+        ]
+        for q in range(CHUNKS):
+            weave(last, q)
+            quantise_page(1, q)
+        for q in range(CHUNKS):
+            for n in range(N_TILES):
+                if q >= early_chunks:
+                    second_product(0, q, n)
+                second_product(1, q, n)
+                dst = staged[q // 2][:, (q % 2) * N_TILES + n, :]
+                if q > 0 and n == 1:
+                    nc.vector.tensor_copy(dst, score_banks[q, n][:])
+                else:
+                    nc.scalar.copy(dst, score_banks[q, n][:])
+                nc.sync.dma_start(out[n * P : (n + 1) * P, q * BANK : (q + 1) * BANK], dst)

@@ -1,6 +1,7 @@
 from contextlib import ExitStack
 
 import concourse.mybir as mybir
+from concourse.masks import make_identity
 
 K, T, S, H, T2, PAIRS, N = 1024, 4096, 1024, 1024, 2048, 512, 512
 FLOPS = 2 * K * H * S + 2 * H * N * T2
@@ -48,15 +49,13 @@ def tile_list_quota_swap_scores_kernel(
 
         table_scales = keep.tile([P, T], U8, name="table_scales", align_bytes=64)
         nc.vector.memset(table_scales[:].bitcast(I32), 0)
+        landed_scales = ring.tile([P, T // 4], I32, name="landed_scales", tag="w1_woven", align_bytes=64)
         for q in range(QUADS):
-            nc.gpsimd.dma_start(
-                table_scales[32 * q : 32 * q + 4 * passes, :].bitcast(I32),
-                tab_scales[:, 4 * q : 4 * q + 4, :].bitcast(I32),
-            )
-        gains = keep.tile([P, passes, PACK], F32, name="gains")
-        nc.scalar.dma_start(gains[:], gain.rearrange("(b p i) -> p b i", p=P, i=PACK))
-        rates = keep.tile([P, passes, PACK], F32, name="rates")
-        nc.scalar.dma_start(rates[:], rate.rearrange("(b p i) -> p b i", p=P, i=PACK))
+            live = slice(32 * q, 32 * q + 4 * passes)
+            nc.sync.dma_start(landed_scales[live, :], tab_scales[:, 4 * q : 4 * q + 4, :].bitcast(I32))
+            nc.vector.tensor_copy(table_scales[live, :].bitcast(I32), landed_scales[live, :])
+        identity = keep.tile([P, P], F32, name="identity")
+        make_identity(nc, identity[:])
         w4_planes = keep.tile([P, passes * N], U8, name="w4_planes", align_bytes=64)
         nc.vector.memset(w4_planes[:].bitcast(I32), 0)
 
@@ -65,7 +64,7 @@ def tile_list_quota_swap_scores_kernel(
         w1_codes, w1_planes = {}, {}
 
         def load_w1(a, b):
-            raw = ring.tile([P, PACK, K_PASS], F32, name="w1_raw")
+            raw = ring.tile([P, PACK, K_PASS], F32, name="w1_raw", tag="rows8k", bufs=7)
             nc.sync.dma_start(
                 raw[:],
                 w1[a * K_PASS : (a + 1) * K_PASS, b * K_PASS : (b + 1) * K_PASS].rearrange("(p j) c -> p j c", j=PACK),
@@ -73,7 +72,7 @@ def tile_list_quota_swap_scores_kernel(
             return raw
 
         def quantise_w1(a, b, raw):
-            woven = ring.tile([P, K_PASS * PACK], BF16, name="w1_woven", align_bytes=64)
+            woven = ring.tile([P, K_PASS * PACK], BF16, name="w1_woven", tag="w1_woven", align_bytes=64)
             nc.scalar.copy(
                 woven[:].rearrange("p (i m j) -> p m i j", i=PACK, j=PACK),
                 raw[:].rearrange("p j (m i) -> p m i j", i=PACK),
@@ -89,8 +88,12 @@ def tile_list_quota_swap_scores_kernel(
             nc.sync.dma_start(words[:].bitcast(I32), tab_words[a].rearrange("p t i -> p (t i)").bitcast(I32))
             table.append(words)
         list2 = load_list(offs2, "list2")
+        gains = keep.tile([P, passes, PACK], F32, name="gains")
+        nc.sync.dma_start(gains[:], gain.rearrange("(b p i) -> p b i", p=P, i=PACK))
 
         seasons, pages, weights = {}, {}, {}
+        halves = [slice(u * BANK, (u + 1) * BANK) for u in range(S // BANK)]
+        whole = slice(0, S)
 
         def rows(src, c):
             b, i = SLICES[c]
@@ -98,36 +101,42 @@ def tile_list_quota_swap_scores_kernel(
 
         def load_slice(c):
             b, i = SLICES[c]
-            seasons[c] = ring.tile([P, S], F32, name="season_rows", bufs=3)
-            nc.sync.dma_start(seasons[c][:], rows(season, c))
+            seasons[c] = ring.tile([P, S], F32, name="season_rows", bufs=4)
+            pages[c] = ring.tile([P, T2], F32, name="page", tag="rows8k", bufs=7)
             if b == 0:
                 weights[i] = keep.tile([P, S], F32, name="wgs_rows_%d" % i)
-                for q in range(QUADS):
-                    nc.sync.dma_start(
-                        weights[i][32 * q : 32 * q + 32, :], wgs.rearrange("(m i) s -> i m s", i=PACK)[i]
-                    )
-            pages[c] = ring.tile([P, T2], F32, name="page", bufs=5)
-            nc.sync.dma_start(pages[c][:], rows(page0, c))
+            for k, cols in enumerate(halves if c == 0 else [whole]):
+                nc.sync.dma_start(seasons[c][:, cols], rows(season, c)[:, cols])
+                if k == 0:
+                    nc.sync.dma_start(pages[c][:], rows(page0, c))
+                if b == 0:
+                    for q in range(QUADS):
+                        nc.sync.dma_start(
+                            weights[i][32 * q : 32 * q + 32, cols],
+                            wgs.rearrange("(m i) s -> i m s", i=PACK)[i][:, cols],
+                        )
 
         load_slice(0)
         list3 = load_list(offs3, "list3")
         list4 = load_list(offs4, "list4")
+        rates = keep.tile([P, passes, PACK], F32, name="rates")
+        nc.sync.dma_start(rates[:], rate.rearrange("(b p i) -> p b i", p=P, i=PACK))
         load_slice(1)
-        load_slice(2)
 
         for a in range(passes):
             quantise_w1(a, 0, raws[a])
+        raws = [load_w1(a, 1) for a in range(passes)]
+        load_slice(2)
 
         picked_scales = keep.tile([P, S], U8, name="picked_scales", align_bytes=64)
         nc.vector.tensor_copy(picked_scales[:], table_scales[:].indirect(list1[:]))
         picked = [keep.tile([P, S], U32, name="picked_words_%d" % a, align_bytes=64) for a in range(passes)]
         nc.vector.tensor_copy(picked[0][:], table[0][:].indirect(list1[:]))
-        halves = [slice(u * BANK, (u + 1) * BANK) for u in range(S // BANK)]
         list_halves = [slice(u * BANK // 16, (u + 1) * BANK // 16) for u in range(S // BANK)]
         for cols, lcols in zip(halves, list_halves):
             nc.vector.tensor_copy(picked[1][:, cols], table[1][:].indirect(list1[:, lcols]))
 
-        tanhs, hs, sides3, sides4, tops, scaled4, scaled_tops = {}, {}, {}, {}, {}, {}, {}
+        tanhs, sides3, sides4, scratch = {}, {}, {}, {}
 
         def first_product(c):
             b, i = SLICES[c]
@@ -149,49 +158,93 @@ def tile_list_quota_swap_scores_kernel(
         def make_h(c, cols):
             b, i = SLICES[c]
             nc.vector.scalar_tensor_tensor(
-                hs[c][:, cols], tanhs[c][:, cols], gains[:, b, i : i + 1], seasons[c][:, cols], ALU.mult, ALU.add
+                seasons[c][:, cols], tanhs[c][:, cols], gains[:, b, i : i + 1], seasons[c][:, cols], ALU.mult, ALU.add
             )
+
+        low, high = halves
+
+        def turn_sum(c):
+            b, i = SLICES[c]
+            for cols in halves:
+                nc.scalar.activation(tanhs[c][:, cols], tanhs[c][:, cols], ACT.Copy, scale=gains[:, b, i : i + 1])
+            for cols in halves:
+                bank = psum.tile([P, BANK], F32, name="bank")
+                for k, term in enumerate((seasons[c], tanhs[c])):
+                    for u in range(BANK // P):
+                        block = slice(cols.start + u * P, cols.start + (u + 1) * P)
+                        nc.tensor.matmul(
+                            bank[:, u * P : (u + 1) * P], term[:, block], identity[:],
+                            start=(k == 0 and u == 0), stop=(k == 1 and u == BANK // P - 1), is_transpose=True,
+                        )
+                nc.scalar.copy(scratch[c - 2][:, cols], bank[:])
+
+        def turn_back(c, cols):
+            bank = psum.tile([P, BANK], F32, name="bank")
+            for u in range(BANK // P):
+                block = slice(cols.start + u * P, cols.start + (u + 1) * P)
+                nc.tensor.transpose(bank[:, u * P : (u + 1) * P], scratch[c - 2][:, block], identity[:])
+            return bank
 
         def put_h(c, cols, lcols):
             i = SLICES[c][1]
             nc.vector.tensor_tensor(
-                pages[c][:].indirect(list2[:, lcols]), hs[c][:, cols], weights[i][:, cols], ALU.mult
+                pages[c][:].indirect(list2[:, lcols]), seasons[c][:, cols], weights[i][:, cols], ALU.mult
             )
 
-        def fetch(c):
-            b, i = SLICES[c]
+        def fetch3(c):
             sides3[c] = ring.tile([P, PAIRS], F32, name="side3")
             nc.vector.tensor_copy(sides3[c][:], pages[c][:].indirect(list3[:]))
+
+        def fetch4(c):
             sides4[c] = ring.tile([P, PAIRS], F32, name="side4")
             nc.vector.tensor_copy(sides4[c][:], pages[c][:].indirect(list4[:]))
-            scaled4[c] = ring.tile([P, PAIRS], F32, name="scaled4")
-            nc.scalar.activation(scaled4[c][:], sides4[c][:], ACT.Copy, scale=rates[:, b, i : i + 1])
+
+        def top(c):
+            return sides3[c][:] if c == last else scratch[c - 1][:, low]
 
         def larger(c):
+            nc.vector.tensor_tensor(top(c), sides3[c][:], sides4[c][:], ALU.max)
+
+        def scale_side4(c):
             b, i = SLICES[c]
-            tops[c] = ring.tile([P, PAIRS], F32, name="top")
-            nc.vector.tensor_tensor(tops[c][:], sides3[c][:], sides4[c][:], ALU.max)
-            scaled_tops[c] = ring.tile([P, PAIRS], F32, name="scaled_top")
-            nc.scalar.activation(scaled_tops[c][:], tops[c][:], ACT.Copy, scale=minus_rates[:, b, i : i + 1])
+            nc.scalar.activation(scratch[c][:, low], sides4[c][:], ACT.Copy, scale=rates[:, b, i : i + 1])
+
+        def scale_top(c):
+            b, i = SLICES[c]
+            nc.scalar.activation(scratch[c][:, high], top(c), ACT.Copy, scale=minus_rates[:, b, i : i + 1])
 
         def put_top(c):
-            nc.vector.tensor_copy(pages[c][:].indirect(list3[:]), tops[c][:])
+            nc.vector.tensor_copy(pages[c][:].indirect(list3[:]), top(c))
 
         def put_shortfall(c):
-            nc.vector.tensor_tensor(pages[c][:].indirect(list4[:]), scaled4[c][:], scaled_tops[c][:], ALU.add)
+            nc.vector.tensor_tensor(pages[c][:].indirect(list4[:]), scratch[c][:, low], scratch[c][:, high], ALU.add)
 
-        woven_page, page_codes, page_planes = {}, {}, {}
+        rounded, woven_page, page_codes, page_planes = {}, {}, {}, {}
 
-        def weave(c, q):
+        def new_woven(b, q):
+            woven_page[b, q] = keep.tile(
+                [P, BANK, PACK], BF16, name="woven_page", tag="woven_page_%d" % q, align_bytes=64
+            )
+
+        def round_page(c, q):
             b, i = SLICES[c]
-            if i == BYTE_ORDER[0]:
-                woven_page[b, q] = keep.tile(
-                    [P, BANK, PACK], BF16, name="woven_page", tag="woven_page_%d" % q, align_bytes=64
-                )
             src = pages[c][:, q * BANK : (q + 1) * BANK]
-            if c == last:
-                nc.vector.tensor_copy(woven_page[b, q][:, :, i], src)
+            if b == 0:
+                if i == 0:
+                    rounded[q] = keep.tile([P, PACK, BANK], BF16, name="rounded_%d" % q)
+                nc.scalar.copy(rounded[q][:, i, :], src)
+                if i == PACK - 1:
+                    new_woven(b, q)
+                    nc.scalar.copy(
+                        woven_page[b, q][:].rearrange("p (t u) i -> p t i u", u=4),
+                        rounded[q][:].rearrange("p i (t u) -> p t i u", u=4),
+                    )
+            elif c == last and q < CHUNKS - 1:
+                for cols in (slice(0, BANK // 2), slice(BANK // 2, BANK)):
+                    nc.vector.tensor_copy(woven_page[b, q][:, cols, i], src[:, cols])
             else:
+                if i == 0:
+                    new_woven(b, q)
                 nc.scalar.copy(woven_page[b, q][:, :, i], src)
 
         def quantise_page(b, q):
@@ -224,20 +277,20 @@ def tile_list_quota_swap_scores_kernel(
         minus_rates = keep.tile([P, passes, PACK], F32, name="minus_rates")
         nc.scalar.mul(minus_rates[:], rates[:], -1.0)
 
-        hs[0] = ring.tile([P, S], F32, name="h_rows")
         for cols in halves:
             make_h(0, cols)
         for cols, lcols in zip(halves, list_halves):
             put_h(0, cols, lcols)
+        fetch3(0)
+        fetch4(0)
 
-        whole = slice(0, S)
         whole_list = slice(0, S // 16)
         early_chunks = 8 // N_TILES
         for c in range(-1, last + 1):
+            scratch[c] = ring.tile([P, S], F32, name="scratch", bufs=3)
             if c + 4 <= last:
                 load_slice(c + 4)
             if c == -1:
-                raws = [load_w1(a, 1) for a in range(passes)]
                 nc.sync.dma_start(
                     w4_codes[:].bitcast(I32), w4_words.bitcast(I32).rearrange("a p n -> p a n")
                 )
@@ -247,30 +300,40 @@ def tile_list_quota_swap_scores_kernel(
                         w4_planes[32 * q : 32 * q + 4, :].bitcast(I32).rearrange("r (a n) -> r a n", a=passes),
                         w4_scales[:, 4 * q : 4 * q + 4, :].bitcast(I32).rearrange("a r n -> r a n"),
                     )
-            if c >= 0:
-                put_top(c)
-            if c + 1 <= last:
-                fetch(c + 1)
             if c + 2 <= last:
-                hs[c + 2] = ring.tile([P, S], F32, name="h_rows")
-                make_h(c + 2, whole)
+                turn_sum(c + 2)
+                banks = [turn_back(c + 2, cols) for cols in halves]
             if c >= 0:
-                put_shortfall(c)
-            if c + 1 <= last:
-                larger(c + 1)
-            if c == 0:
-                for a in range(passes):
-                    quantise_w1(a, 1, raws[a])
+                scale_side4(c)
+            if c + 2 <= last:
+                nc.scalar.copy(seasons[c + 2][:, low], banks[0][:])
+            if c >= 0:
+                scale_top(c)
+            if c + 2 <= last:
+                nc.scalar.copy(seasons[c + 2][:, high], banks[1][:])
             if c + 3 <= last:
                 first_product(c + 3)
+            if c >= 1:
+                for q in range(CHUNKS):
+                    round_page(c - 1, q)
+            if c >= 0:
+                put_shortfall(c)
+            if c + 2 <= last:
+                put_h(c + 2, whole, whole_list)
+            if c + 1 <= last:
+                larger(c + 1)
+            if c + 2 <= last:
+                fetch3(c + 2)
+            if c + 1 <= last:
+                put_top(c + 1)
+            if c + 2 <= last:
+                fetch4(c + 2)
+            if c == -1:
+                for a in range(passes):
+                    quantise_w1(a, 1, raws[a])
             if c == PACK:
                 for q in range(CHUNKS):
                     quantise_page(0, q)
-            if c + 2 <= last:
-                put_h(c + 2, whole, whole_list)
-            if 0 <= c < last:
-                for q in range(CHUNKS):
-                    weave(c, q)
             if c == PACK + 1:
                 for q in range(early_chunks):
                     for n in range(N_TILES):
@@ -280,16 +343,21 @@ def tile_list_quota_swap_scores_kernel(
             ring.tile([P, 2 * N_TILES, BANK], F32, name="staged", tag="wide", align_bytes=64) for u in range(2)
         ]
         for q in range(CHUNKS):
-            weave(last, q)
+            round_page(last, q)
             quantise_page(1, q)
         for q in range(CHUNKS):
             for n in range(N_TILES):
                 if q >= early_chunks:
                     second_product(0, q, n)
                 second_product(1, q, n)
-                dst = staged[q // 2][:, (q % 2) * N_TILES + n, :]
-                if q > 0 and n == 1:
-                    nc.vector.tensor_copy(dst, score_banks[q, n][:])
+                slot = (q % 2) * N_TILES + n
+                if q > 0 and n == 1 or q == CHUNKS - 1 and n == 3:
+                    nc.vector.tensor_copy(staged[q // 2][:, slot, :], score_banks[q, n][:])
                 else:
-                    nc.scalar.copy(dst, score_banks[q, n][:])
-                nc.sync.dma_start(out[n * P : (n + 1) * P, q * BANK : (q + 1) * BANK], dst)
+                    nc.scalar.copy(staged[q // 2][:, slot, :], score_banks[q, n][:])
+                step = 1 if q == 0 else 2
+                if (n + 1) % step == 0:
+                    nc.sync.dma_start(
+                        out.rearrange("(n p) t -> p n t", p=P)[:, n + 1 - step : n + 1, q * BANK : (q + 1) * BANK],
+                        staged[q // 2][:, slot + 1 - step : slot + 1, :],
+                    )

@@ -219,11 +219,13 @@ def tile_list_quota_swap_scores_kernel(
         def put_shortfall(c):
             nc.vector.tensor_tensor(pages[c][:].indirect(list4[:]), scratch[c][:, low], scratch[c][:, high], ALU.add)
 
+        whole_chunk = slice(0, BANK)
+        half_chunks = [slice(0, BANK // 2), slice(BANK // 2, BANK)]
         rounded, woven_page, page_codes, page_planes = {}, {}, {}, {}
 
         def new_woven(b, q):
             woven_page[b, q] = keep.tile(
-                [P, BANK, PACK], BF16, name="woven_page", tag="woven_page_%d" % q, align_bytes=64
+                [P, BANK, PACK], BF16, name="woven_page", tag="page_bf16_%d_%d" % (b, q), align_bytes=64
             )
 
         def round_page(c, q):
@@ -231,7 +233,9 @@ def tile_list_quota_swap_scores_kernel(
             src = pages[c][:, q * BANK : (q + 1) * BANK]
             if b == 0:
                 if i == 0:
-                    rounded[q] = keep.tile([P, PACK, BANK], BF16, name="rounded_%d" % q)
+                    rounded[q] = keep.tile(
+                        [P, PACK, BANK], BF16, name="rounded", tag="page_bf16_1_%d" % q, align_bytes=64
+                    )
                 nc.scalar.copy(rounded[q][:, i, :], src)
                 if i == PACK - 1:
                     new_woven(b, q)
@@ -239,38 +243,44 @@ def tile_list_quota_swap_scores_kernel(
                         woven_page[b, q][:].rearrange("p (t u) i -> p t i u", u=4),
                         rounded[q][:].rearrange("p i (t u) -> p t i u", u=4),
                     )
-            elif c == last and q < CHUNKS - 1:
-                for cols in (slice(0, BANK // 2), slice(BANK // 2, BANK)):
-                    nc.vector.tensor_copy(woven_page[b, q][:, cols, i], src[:, cols])
             else:
                 if i == 0:
                     new_woven(b, q)
                 nc.scalar.copy(woven_page[b, q][:, :, i], src)
 
-        def quantise_page(b, q):
-            page_codes[b, q] = keep.tile([P, BANK], U32, name="page_codes_%d%d" % (b, q), align_bytes=64)
-            page_planes[b, q] = keep.tile([P, BANK], U8, name="page_planes_%d%d" % (b, q), align_bytes=64)
+        def quantise_page(b, q, codes, cols):
+            if cols.start == 0:
+                page_codes[b, q] = codes
+                page_planes[b, q] = keep.tile([P, BANK], U8, name="page_planes_%d%d" % (b, q), align_bytes=64)
             nc.vector.quantize_mx(
-                page_codes[b, q][:].bitcast(FP8X4),
-                page_planes[b, q][:],
-                woven_page[b, q][:].rearrange("p t i -> p (t i)"),
+                page_codes[b, q][:, cols].bitcast(FP8X4),
+                page_planes[b, q][:, cols],
+                woven_page[b, q][:, cols, :].rearrange("p t i -> p (t i)"),
             )
 
         w4_codes = keep.tile([P, passes, 2 * N], U8, name="w4_codes", align_bytes=64)
         score_banks = {}
 
-        def second_product(b, q, n):
+        def bank_sums(q, k):
+            if q == 0:
+                return [(2 * (k % 2) + j, half_chunks[k // 2]) for j in range(2)]
+            return [(k, whole_chunk)]
+
+        def second_product(b, q, k):
             if b == 0:
-                score_banks[q, n] = psum.tile([P, BANK], F32, name="bank")
-            nc.tensor.matmul_mx(
-                score_banks[q, n][:],
-                lhsT=w4_codes[:, b, 2 * P * n : 2 * P * (n + 1)].bitcast(FP4X4),
-                lhsT_scale=w4_planes[:, b * N + P * n : b * N + P * (n + 1)],
-                rhs=page_codes[b, q][:].bitcast(FP8X4),
-                rhs_scale=page_planes[b, q][:],
-                start=(b == 0),
-                stop=(b == passes - 1),
-            )
+                score_banks[q, k] = psum.tile([P, BANK], F32, name="bank")
+            sums = bank_sums(q, k)
+            width = BANK // len(sums)
+            for j, (n, cols) in enumerate(sums):
+                nc.tensor.matmul_mx(
+                    score_banks[q, k][:, j * width : (j + 1) * width],
+                    lhsT=w4_codes[:, b, 2 * P * n : 2 * P * (n + 1)].bitcast(FP4X4),
+                    lhsT_scale=w4_planes[:, b * N + P * n : b * N + P * (n + 1)],
+                    rhs=page_codes[b, q][:, cols].bitcast(FP8X4),
+                    rhs_scale=page_planes[b, q][:, cols],
+                    start=(b == 0 and j == 0),
+                    stop=(b == passes - 1 and j == len(sums) - 1),
+                )
 
         first_product(0)
         first_product(1)
@@ -287,7 +297,7 @@ def tile_list_quota_swap_scores_kernel(
         whole_list = slice(0, S // 16)
         early_chunks = 8 // N_TILES
         for c in range(-1, last + 1):
-            scratch[c] = ring.tile([P, S], F32, name="scratch", bufs=3)
+            scratch[c] = ring.tile([P, S], F32, name="scratch", tag="scratch", bufs=3, align_bytes=64)
             if c + 4 <= last:
                 load_slice(c + 4)
             if c == -1:
@@ -331,33 +341,54 @@ def tile_list_quota_swap_scores_kernel(
             if c == -1:
                 for a in range(passes):
                     quantise_w1(a, 1, raws[a])
-            if c == PACK:
-                for q in range(CHUNKS):
-                    quantise_page(0, q)
-            if c == PACK + 1:
-                for q in range(early_chunks):
-                    for n in range(N_TILES):
-                        second_product(0, q, n)
+
+        for q in range(early_chunks):
+            codes = ring.tile([P, BANK], U32, name="early_codes", tag="scratch", bufs=3, align_bytes=64)
+            quantise_page(0, q, codes[:], whole_chunk)
+            for n in range(N_TILES):
+                second_product(0, q, n)
+        late_codes = ring.tile([P, 2 * BANK], U32, name="late_codes", tag="scratch", bufs=3, align_bytes=64)
 
         staged = [
             ring.tile([P, 2 * N_TILES, BANK], F32, name="staged", tag="wide", align_bytes=64) for u in range(2)
         ]
+        last_byte = SLICES[last][1]
+        round_page(last, CHUNKS - 1)
         for q in range(CHUNKS):
-            round_page(last, q)
-            quantise_page(1, q)
+            if q >= early_chunks:
+                quantise_page(0, q, late_codes[:, halves[q - early_chunks]], whole_chunk)
+            codes = keep.tile([P, BANK], U32, name="page_codes_%d" % q, align_bytes=64)
+            for cols in half_chunks:
+                if q < CHUNKS - 1:
+                    nc.vector.tensor_copy(
+                        woven_page[1, q][:, cols, last_byte], pages[last][:, q * BANK : (q + 1) * BANK][:, cols]
+                    )
+                if q == 0:
+                    quantise_page(1, q, codes[:], cols)
+            if q > 0:
+                quantise_page(1, q, codes[:], whole_chunk)
+        scores = out.rearrange("(n p) t -> p n t", p=P)
         for q in range(CHUNKS):
-            for n in range(N_TILES):
-                if q >= early_chunks:
-                    second_product(0, q, n)
-                second_product(1, q, n)
-                slot = (q % 2) * N_TILES + n
-                if q > 0 and n == 1 or q == CHUNKS - 1 and n == 3:
-                    nc.vector.tensor_copy(staged[q // 2][:, slot, :], score_banks[q, n][:])
+            if q == early_chunks:
+                for k in range(N_TILES):
+                    second_product(0, q, k)
+            for k in range(N_TILES):
+                if q > early_chunks:
+                    second_product(0, q, k)
+                second_product(1, q, k)
+                slot = (q % 2) * N_TILES + k
+                if q >= early_chunks and k % 2 == 1:
+                    nc.vector.tensor_copy(staged[q // 2][:, slot, :], score_banks[q, k][:])
                 else:
-                    nc.scalar.copy(staged[q // 2][:, slot, :], score_banks[q, n][:])
-                step = 1 if q == 0 else 2
-                if (n + 1) % step == 0:
+                    nc.scalar.copy(staged[q // 2][:, slot, :], score_banks[q, k][:])
+                if q == 0:
+                    (n, cols), other = bank_sums(q, k)
                     nc.sync.dma_start(
-                        out.rearrange("(n p) t -> p n t", p=P)[:, n + 1 - step : n + 1, q * BANK : (q + 1) * BANK],
-                        staged[q // 2][:, slot + 1 - step : slot + 1, :],
+                        scores[:, n : n + 2, cols], staged[0][:, slot, :].rearrange("p (n t) -> p n t", n=2)
+                    )
+                elif q == CHUNKS - 1:
+                    nc.sync.dma_start(scores[:, k, q * BANK : (q + 1) * BANK], staged[q // 2][:, slot, :])
+                elif k % 2 == 1:
+                    nc.sync.dma_start(
+                        scores[:, k - 1 : k + 1, q * BANK : (q + 1) * BANK], staged[q // 2][:, slot - 1 : slot + 1, :]
                     )

from contextlib import ExitStack

import concourse.mybir as mybir
from concourse.masks import make_identity

K, T, S, H, T2, PAIRS, N = 1024, 4096, 1024, 1024, 2048, 512, 512
FLOPS = 2 * K * H * S + 2 * H * N * T2

F32 = mybir.dt.float32
BF16 = mybir.dt.bfloat16
I32 = mybir.dt.int32
U32 = mybir.dt.uint32
U16 = mybir.dt.uint16
U8 = mybir.dt.uint8
FP8X4 = mybir.dt.float8_e4m3fn_x4
FP4X4 = mybir.dt.float4_e2m1fn_x4
ALU = mybir.AluOpType
ACT = mybir.ActivationFunctionType

P = 128
PACK = 4
K_PASS = P * PACK
BANK = 512
QUADS = 4
BYTE_ORDER = (0, 2, 1, 3)
SLICES = [(b, i) for b in range(H // K_PASS) for i in BYTE_ORDER]
CHUNKS = T2 // BANK
N_TILES = N // P
VECTOR_BANKS = 3


def tile_list_quota_swap_scores_kernel(
    tc, tab_words, tab_scales, w1, gain, season, page0, wgs, rate,
    w4_words, w4_scales, offs, offs2, offs3, offs4, out,
):
    nc = tc.nc
    passes = K // K_PASS
    last = len(SLICES) - 1

    with ExitStack() as ctx:
        keep = ctx.enter_context(tc.tile_pool(name="keep", bufs=1))
        ring = ctx.enter_context(tc.tile_pool(name="ring", bufs=2))
        psum = ctx.enter_context(tc.psum_pool(name="psum", bufs=8))

        def load_list(src, name):
            tile = keep.tile(list(src.shape), U16, name=name)
            nc.sync.dma_start(tile[:], src)
            return tile

        table_scales = keep.tile([P, T], U8, name="table_scales", align_bytes=64)
        nc.vector.memset(table_scales[:].bitcast(I32), 0)
        landed_scales = ring.tile([P, T // 4], I32, name="landed_scales", tag="w1_woven", align_bytes=64)
        for q in range(QUADS):
            live = slice(32 * q, 32 * q + 4 * passes)
            nc.sync.dma_start(landed_scales[live, :], tab_scales[:, 4 * q : 4 * q + 4, :].bitcast(I32))
            nc.vector.tensor_copy(table_scales[live, :].bitcast(I32), landed_scales[live, :])
        identity = keep.tile([P, P], F32, name="identity")
        make_identity(nc, identity[:])
        w4_planes = keep.tile([P, passes * N], U8, name="w4_planes", align_bytes=64)
        nc.vector.memset(w4_planes[:].bitcast(I32), 0)

        list1 = load_list(offs, "list1")

        w1_codes, w1_planes = {}, {}

        def load_w1(a, b):
            raw = ring.tile([P, PACK, K_PASS], F32, name="w1_raw", tag="rows8k", bufs=7)
            nc.sync.dma_start(
                raw[:],
                w1[a * K_PASS : (a + 1) * K_PASS, b * K_PASS : (b + 1) * K_PASS].rearrange("(p j) c -> p j c", j=PACK),
            )
            return raw

        def quantise_w1(a, b, raw):
            woven = ring.tile([P, K_PASS * PACK], BF16, name="w1_woven", tag="w1_woven", align_bytes=64)
            nc.scalar.copy(
                woven[:].rearrange("p (i m j) -> p m i j", i=PACK, j=PACK),
                raw[:].rearrange("p j (m i) -> p m i j", i=PACK),
            )
            w1_codes[a, b] = keep.tile([P, K_PASS], U32, name="w1_codes_%d%d" % (a, b), align_bytes=64)
            w1_planes[a, b] = keep.tile([P, K_PASS], U8, name="w1_planes_%d%d" % (a, b), align_bytes=64)
            nc.vector.quantize_mx(w1_codes[a, b][:].bitcast(FP8X4), w1_planes[a, b][:], woven[:])

        raws = [load_w1(a, 0) for a in range(passes)]
        table = []
        for a in range(passes):
            words = ring.tile([P, T], U32, name="table_words", tag="wide", align_bytes=64)
            nc.sync.dma_start(words[:].bitcast(I32), tab_words[a].rearrange("p t i -> p (t i)").bitcast(I32))
            table.append(words)
        list2 = load_list(offs2, "list2")
        gains = keep.tile([P, passes, PACK], F32, name="gains")
        nc.sync.dma_start(gains[:], gain.rearrange("(b p i) -> p b i", p=P, i=PACK))

        seasons, pages, weights = {}, {}, {}
        halves = [slice(u * BANK, (u + 1) * BANK) for u in range(S // BANK)]
        whole = slice(0, S)

        def rows(src, c):
            b, i = SLICES[c]
            return src.rearrange("(b p i) s -> b i p s", p=P, i=PACK)[b, i]

        def load_slice(c):
            b, i = SLICES[c]
            seasons[c] = ring.tile([P, S], F32, name="season_rows", bufs=4)
            pages[c] = ring.tile([P, T2], F32, name="page", tag="rows8k", bufs=7)
            if b == 0:
                weights[i] = keep.tile([P, S], F32, name="wgs_rows_%d" % i)
            for k, cols in enumerate(halves if c == 0 else [whole]):
                nc.sync.dma_start(seasons[c][:, cols], rows(season, c)[:, cols])
                if k == 0:
                    nc.sync.dma_start(pages[c][:], rows(page0, c))
                if b == 0:
                    for q in range(QUADS):
                        nc.sync.dma_start(
                            weights[i][32 * q : 32 * q + 32, cols],
                            wgs.rearrange("(m i) s -> i m s", i=PACK)[i][:, cols],
                        )

        load_slice(0)
        list3 = load_list(offs3, "list3")
        list4 = load_list(offs4, "list4")
        rates = keep.tile([P, passes, PACK], F32, name="rates")
        nc.sync.dma_start(rates[:], rate.rearrange("(b p i) -> p b i", p=P, i=PACK))
        load_slice(1)

        for a in range(passes):
            quantise_w1(a, 0, raws[a])
        raws = [load_w1(a, 1) for a in range(passes)]
        load_slice(2)

        picked_scales = keep.tile([P, S], U8, name="picked_scales", align_bytes=64)
        nc.vector.tensor_copy(picked_scales[:], table_scales[:].indirect(list1[:]))
        picked = [keep.tile([P, S], U32, name="picked_words_%d" % a, align_bytes=64) for a in range(passes)]
        nc.vector.tensor_copy(picked[0][:], table[0][:].indirect(list1[:]))
        list_halves = [slice(u * BANK // 16, (u + 1) * BANK // 16) for u in range(S // BANK)]
        for cols, lcols in zip(halves, list_halves):
            nc.vector.tensor_copy(picked[1][:, cols], table[1][:].indirect(list1[:, lcols]))

        tanhs, sides3, sides4, scratch = {}, {}, {}, {}

        def first_product(c):
            b, i = SLICES[c]
            tanhs[c] = ring.tile([P, S], F32, name="tanh_rows")
            for cols in halves:
                bank = psum.tile([P, BANK], F32, name="bank")
                for a in range(passes):
                    nc.tensor.matmul_mx(
                        bank[:],
                        lhsT=w1_codes[a, b][:, i * P : (i + 1) * P].bitcast(FP8X4),
                        lhsT_scale=w1_planes[a, b][:, i * P : (i + 1) * P],
                        rhs=picked[a][:, cols].bitcast(FP8X4),
                        rhs_scale=picked_scales[4 * a : P, cols],
                        start=(a == 0),
                        stop=(a == passes - 1),
                    )
                nc.scalar.activation(tanhs[c][:, cols], bank[:], ACT.Tanh)

        def make_h(c, cols):
            b, i = SLICES[c]
            nc.vector.scalar_tensor_tensor(
                seasons[c][:, cols], tanhs[c][:, cols], gains[:, b, i : i + 1], seasons[c][:, cols], ALU.mult, ALU.add
            )

        low, high = halves

        def turn_sum(c):
            b, i = SLICES[c]
            for cols in halves:
                nc.scalar.activation(tanhs[c][:, cols], tanhs[c][:, cols], ACT.Copy, scale=gains[:, b, i : i + 1])
            for cols in halves:
                bank = psum.tile([P, BANK], F32, name="bank")
                for k, term in enumerate((seasons[c], tanhs[c])):
                    for u in range(BANK // P):
                        block = slice(cols.start + u * P, cols.start + (u + 1) * P)
                        nc.tensor.matmul(
                            bank[:, u * P : (u + 1) * P], term[:, block], identity[:],
                            start=(k == 0 and u == 0), stop=(k == 1 and u == BANK // P - 1), is_transpose=True,
                        )
                nc.scalar.copy(scratch[c - 2][:, cols], bank[:])

        def turn_back(c, cols):
            bank = psum.tile([P, BANK], F32, name="bank")
            for u in range(BANK // P):
                block = slice(cols.start + u * P, cols.start + (u + 1) * P)
                nc.tensor.transpose(bank[:, u * P : (u + 1) * P], scratch[c - 2][:, block], identity[:])
            return bank

        def put_h(c, cols, lcols):
            i = SLICES[c][1]
            nc.vector.tensor_tensor(
                pages[c][:].indirect(list2[:, lcols]), seasons[c][:, cols], weights[i][:, cols], ALU.mult
            )

        def fetch3(c):
            sides3[c] = ring.tile([P, PAIRS], F32, name="side3")
            nc.vector.tensor_copy(sides3[c][:], pages[c][:].indirect(list3[:]))

        def fetch4(c):
            sides4[c] = ring.tile([P, PAIRS], F32, name="side4")
            nc.vector.tensor_copy(sides4[c][:], pages[c][:].indirect(list4[:]))

        def top(c):
            return sides3[c][:] if c == last else scratch[c - 1][:, low]

        def larger(c):
            nc.vector.tensor_tensor(top(c), sides3[c][:], sides4[c][:], ALU.max)

        def scale_side4(c):
            b, i = SLICES[c]
            nc.scalar.activation(scratch[c][:, low], sides4[c][:], ACT.Copy, scale=rates[:, b, i : i + 1])

        def scale_top(c):
            b, i = SLICES[c]
            nc.scalar.activation(scratch[c][:, high], top(c), ACT.Copy, scale=minus_rates[:, b, i : i + 1])

        def put_top(c):
            nc.vector.tensor_copy(pages[c][:].indirect(list3[:]), top(c))

        def put_shortfall(c):
            nc.vector.tensor_tensor(pages[c][:].indirect(list4[:]), scratch[c][:, low], scratch[c][:, high], ALU.add)

        whole_chunk = slice(0, BANK)
        half_chunks = [slice(0, BANK // 2), slice(BANK // 2, BANK)]
        rounded, woven_page, page_codes, page_planes = {}, {}, {}, {}

        def new_woven(b, q):
            woven_page[b, q] = keep.tile(
                [P, BANK, PACK], BF16, name="woven_page", tag="page_bf16_%d_%d" % (b, q), align_bytes=64
            )

        def round_page(c, q):
            b, i = SLICES[c]
            src = pages[c][:, q * BANK : (q + 1) * BANK]
            if b == 0:
                if i == 0:
                    rounded[q] = keep.tile(
                        [P, PACK, BANK], BF16, name="rounded", tag="page_bf16_1_%d" % q, align_bytes=64
                    )
                nc.scalar.copy(rounded[q][:, i, :], src)
                if i == PACK - 1:
                    new_woven(b, q)
                    nc.scalar.copy(
                        woven_page[b, q][:].rearrange("p (t u) i -> p t i u", u=4),
                        rounded[q][:].rearrange("p i (t u) -> p t i u", u=4),
                    )
            else:
                if i == 0:
                    new_woven(b, q)
                nc.scalar.copy(woven_page[b, q][:, :, i], src)

        def quantise_page(b, q, codes, cols):
            if cols.start == 0:
                page_codes[b, q] = codes
                page_planes[b, q] = keep.tile([P, BANK], U8, name="page_planes_%d%d" % (b, q), align_bytes=64)
            nc.vector.quantize_mx(
                page_codes[b, q][:, cols].bitcast(FP8X4),
                page_planes[b, q][:, cols],
                woven_page[b, q][:, cols, :].rearrange("p t i -> p (t i)"),
            )

        w4_codes = keep.tile([P, passes, 2 * N], U8, name="w4_codes", align_bytes=64)
        score_banks = {}

        def bank_sums(q, k):
            if q == 0:
                return [(2 * (k % 2) + j, half_chunks[k // 2]) for j in range(2)]
            return [(k, whole_chunk)]

        def second_product(b, q, k):
            if b == 0:
                score_banks[q, k] = psum.tile([P, BANK], F32, name="bank")
            sums = bank_sums(q, k)
            width = BANK // len(sums)
            for j, (n, cols) in enumerate(sums):
                nc.tensor.matmul_mx(
                    score_banks[q, k][:, j * width : (j + 1) * width],
                    lhsT=w4_codes[:, b, 2 * P * n : 2 * P * (n + 1)].bitcast(FP4X4),
                    lhsT_scale=w4_planes[:, b * N + P * n : b * N + P * (n + 1)],
                    rhs=page_codes[b, q][:, cols].bitcast(FP8X4),
                    rhs_scale=page_planes[b, q][:, cols],
                    start=(b == 0 and j == 0),
                    stop=(b == passes - 1 and j == len(sums) - 1),
                )

        first_product(0)
        first_product(1)
        minus_rates = keep.tile([P, passes, PACK], F32, name="minus_rates")
        nc.scalar.mul(minus_rates[:], rates[:], -1.0)

        for cols in halves:
            make_h(0, cols)
        for cols, lcols in zip(halves, list_halves):
            put_h(0, cols, lcols)
        fetch3(0)
        fetch4(0)

        whole_list = slice(0, S // 16)
        early_chunks = 8 // N_TILES
        for c in range(-1, last + 1):
            scratch[c] = ring.tile([P, S], F32, name="scratch", tag="scratch", bufs=3, align_bytes=64)
            if c + 4 <= last:
                load_slice(c + 4)
            if c == -1:
                nc.sync.dma_start(
                    w4_codes[:].bitcast(I32), w4_words.bitcast(I32).rearrange("a p n -> p a n")
                )
            if c == 1:
                for q in range(QUADS):
                    nc.sync.dma_start(
                        w4_planes[32 * q : 32 * q + 4, :].bitcast(I32).rearrange("r (a n) -> r a n", a=passes),
                        w4_scales[:, 4 * q : 4 * q + 4, :].bitcast(I32).rearrange("a r n -> r a n"),
                    )
            if c + 2 <= last:
                turn_sum(c + 2)
                banks = [turn_back(c + 2, cols) for cols in halves]
            if c >= 0:
                scale_side4(c)
            if c + 2 <= last:
                nc.scalar.copy(seasons[c + 2][:, low], banks[0][:])
            if c >= 0:
                scale_top(c)
            if c + 2 <= last:
                nc.scalar.copy(seasons[c + 2][:, high], banks[1][:])
            if c + 3 <= last:
                first_product(c + 3)
            if c >= 1:
                for q in range(CHUNKS):
                    round_page(c - 1, q)
            if c >= 0:
                put_shortfall(c)
            if c + 2 <= last:
                put_h(c + 2, whole, whole_list)
            if c + 1 <= last:
                larger(c + 1)
            if c + 2 <= last:
                fetch3(c + 2)
            if c + 1 <= last:
                put_top(c + 1)
            if c + 2 <= last:
                fetch4(c + 2)
            if c == -1:
                for a in range(passes):
                    quantise_w1(a, 1, raws[a])

        for q in range(early_chunks):
            codes = ring.tile([P, BANK], U32, name="early_codes", tag="scratch", bufs=3, align_bytes=64)
            quantise_page(0, q, codes[:], whole_chunk)
            for n in range(N_TILES):
                second_product(0, q, n)
        late_codes = ring.tile([P, 2 * BANK], U32, name="late_codes", tag="scratch", bufs=3, align_bytes=64)

        staged = [
            ring.tile([P, 2 * N_TILES, BANK], F32, name="staged", tag="wide", align_bytes=64) for u in range(2)
        ]
        last_byte = SLICES[last][1]
        round_page(last, CHUNKS - 1)
        for q in range(CHUNKS):
            if q >= early_chunks:
                quantise_page(0, q, late_codes[:, halves[q - early_chunks]], whole_chunk)
            codes = keep.tile([P, BANK], U32, name="page_codes_%d" % q, align_bytes=64)
            for cols in half_chunks:
                if q < CHUNKS - 1:
                    nc.vector.tensor_copy(
                        woven_page[1, q][:, cols, last_byte], pages[last][:, q * BANK : (q + 1) * BANK][:, cols]
                    )
                if q == 0:
                    quantise_page(1, q, codes[:], cols)
            if q > 0:
                quantise_page(1, q, codes[:], whole_chunk)
        scores = out.rearrange("(n p) t -> p n t", p=P)
        for q in range(CHUNKS):
            if q == early_chunks:
                for k in range(N_TILES):
                    second_product(0, q, k)
            for k in range(N_TILES):
                if q > early_chunks:
                    second_product(0, q, k)
                second_product(1, q, k)
                slot = (q % 2) * N_TILES + k
                if q >= early_chunks and k % 2 == 1:
                    nc.vector.tensor_copy(staged[q // 2][:, slot, :], score_banks[q, k][:])
                else:
                    nc.scalar.copy(staged[q // 2][:, slot, :], score_banks[q, k][:])
                if q == 0:
                    (n, cols), other = bank_sums(q, k)
                    nc.sync.dma_start(
                        scores[:, n : n + 2, cols], staged[0][:, slot, :].rearrange("p (n t) -> p n t", n=2)
                    )
                elif q == CHUNKS - 1:
                    nc.sync.dma_start(scores[:, k, q * BANK : (q + 1) * BANK], staged[q // 2][:, slot, :])
                elif k % 2 == 1:
                    nc.sync.dma_start(
                        scores[:, k - 1 : k + 1, q * BANK : (q + 1) * BANK], staged[q // 2][:, slot - 1 : slot + 1, :]
                    )
